import numpy as np
import ml_dtypes


def mxq(x, axis, fmt="e4m3"):
    dtype, down = {"e4m3": (ml_dtypes.float8_e4m3fn, 7), "e5m2": (ml_dtypes.float8_e5m2, 14)}[fmt]
    v = np.moveaxis(np.asarray(x, np.float32).astype(ml_dtypes.bfloat16).astype(np.float64), axis, -1)
    blocks = v.reshape(v.shape[:-1] + (-1, 32))
    amax = np.abs(blocks).max(-1, keepdims=True)
    byte = np.maximum(np.where(amax > 0, np.frexp(amax)[1] - 1 + 127, 0) - down, 1)
    scale = np.exp2(byte - 127.0)
    codes = (blocks / scale).astype(np.float32).astype(dtype).astype(np.float64)
    return np.moveaxis((codes * scale).reshape(v.shape), -1, axis)


WIDE = False


def mx_kscale(k):
    if not WIDE:
        return np.ones(k)
    levels = np.array([10, -10, 5, -5, 0])
    if k % 512:
        return np.exp2(np.random.permutation(np.resize(levels, k // 32))).repeat(32)
    a = np.empty((k // 512, 16))
    for p in range(k // 512):
        a[p, :8] = np.random.permutation(np.resize(levels, 8))
        for g in range(8):
            far = levels[np.abs(levels - a[p, g]) >= 10]
            a[p, g + 8] = far[np.random.randint(len(far))]
    return np.exp2(a.ravel()).repeat(32)


def f64(x):
    return np.asarray(x).astype(np.float64)


def striped(idx):
    return np.tile(idx.reshape(-1, 16).T, (8, 1)).astype(np.uint16)


def unstriped(offs):
    return offs[:16].T.reshape(-1).astype(np.int64)


E2M1 = np.array([0.0, 0.5, 1.0, 1.5, 2.0, 3.0, 4.0, 6.0, -0.0, -0.5, -1.0, -1.5, -2.0, -3.0, -4.0, -6.0])


def pack_weight(w, fmt):
    k, n = w.shape
    w = f64(np.asarray(w, np.float32).astype(ml_dtypes.bfloat16)).reshape(k // 32, 32, n)
    amax = np.abs(w).max(1)
    if fmt == "e4m3":
        byte = np.frexp(amax)[1] - 1 + 127 - 7
    else:
        mant, ex = np.frexp(amax / 6.0)
        byte = np.where(mant > 0.5, ex, ex - 1) + 127
    byte = np.clip(np.where(amax > 0, byte, 1), 1, 254)
    scaled = (w * np.exp2(127.0 - byte)[:, None, :]).reshape(k, n).astype(np.float32)
    by_word = np.ascontiguousarray(scaled.reshape(k // 512, 128, 4, n).transpose(0, 1, 3, 2))
    if fmt == "e4m3":
        words = by_word.astype(ml_dtypes.float8_e4m3fn).view(np.uint8)
    else:
        c = by_word.astype(ml_dtypes.float4_e2m1fn).view(np.uint8) & 0xF
        words = (c[..., 0::2] | (c[..., 1::2] << 4)).reshape(k // 512, 128, 2 * n)
    return np.ascontiguousarray(words), np.ascontiguousarray(byte.astype(np.uint8).reshape(k // 512, 16, n))


def unpack_weight(words, scales, fmt):
    g, _, n = scales.shape
    words = np.ascontiguousarray(words).reshape(g, 128, n, -1)
    if fmt == "e4m3":
        vals = words.view(ml_dtypes.float8_e4m3fn).astype(np.float64)
    else:
        nib = np.empty((g, 128, n, 4), np.uint8)
        nib[..., 0::2] = words & 0xF
        nib[..., 1::2] = words >> 4
        vals = E2M1[nib]
    vals = vals * np.repeat(np.exp2(scales.astype(np.float64) - 127.0), 8, axis=1)[..., None]
    return vals.transpose(0, 1, 3, 2).reshape(g * 512, n)


def gelu(v):
    return 0.5 * v * (1.0 + np.tanh(np.sqrt(2.0 / np.pi) * (v + 0.044715 * v**3)))


K, KA, T, S, H, T2, T3, S2, P = 1024, 512, 2048, 512, 1024, 1024, 2048, 1024, 512


def setup_inputs():
    n = np.random.standard_normal
    s = mx_kscale(K)[:, None]
    u = mx_kscale(H)[:, None]
    tab_words, tab_scales = pack_weight(n((K, T)) * s, "e4m3")
    w4_words, w4_scales = pack_weight(0.38 * n((K - KA, H)) / np.sqrt(K) / s[KA:], "e2m1")
    tab2_words, tab2_scales = pack_weight(n((H, T3)) / np.sqrt(H) / u, "e4m3")
    return {
        "tab_words": tab_words, "tab_scales": tab_scales,
        "offs": striped(np.random.permutation(T)[:S]),
        "w1": (0.38 * n((KA, H)) / np.sqrt(K) / s[:KA]).astype(np.float32),
        "w4_words": w4_words, "w4_scales": w4_scales,
        "b1": np.random.uniform(-0.9, 0.9, H).astype(np.float32),
        "gain": (np.random.uniform(0.8, 2.2, H) * u[:, 0]).astype(np.float32),
        "page0": (n((H, T2)) * u).astype(np.float32),
        "wgs": np.exp(0.3 * n((128, S))).astype(np.float32),
        "offs3": striped(np.random.permutation(T2)[:S]),
        "tab2_words": tab2_words, "tab2_scales": tab2_scales,
        "offs2": striped(np.random.permutation(T3)[:S2]),
        "pos1": striped(np.random.permutation(T2)[:P]),
        "pos2": striped(np.random.permutation(T2)[:P]),
        "vis": np.random.uniform(0.2, 1.8, (S2, P)).astype(np.float32),
    }


def reference(tab_words, tab_scales, offs, w1, w4_words, w4_scales, b1, gain, page0, wgs, offs3,
              tab2_words, tab2_scales, offs2, pos1, pos2, vis):
    v = unpack_weight(tab_words, tab_scales, "e4m3")[:, unstriped(offs)]
    v2 = unpack_weight(tab2_words, tab2_scales, "e4m3")[:, unstriped(offs2)]
    w1q = mxq(f64(w1), 0, "e4m3")
    w4 = unpack_weight(w4_words, w4_scales, "e2m1")
    x = w1q.T @ v[:KA] + w4.T @ v[KA:]
    h = np.sin(x + f64(b1)[:, None]) * f64(gain)[:, None]
    page = f64(page0).copy()
    page[:, unstriped(offs3)] = np.tile(f64(wgs), (H // 128, 1)) * h
    e = v2.T @ mxq(page, 0, "e4m3")
    deeper = np.maximum(e[:, unstriped(pos1)], e[:, unstriped(pos2)])
    return deeper * f64(vis)

@@ -1,0 +1,227 @@
+from contextlib import ExitStack
+
+import concourse.mybir as mybir
+
+F32 = mybir.dt.float32
+BF16 = mybir.dt.bfloat16
+I32 = mybir.dt.int32
+U32 = mybir.dt.uint32
+U16 = mybir.dt.uint16
+U8 = mybir.dt.uint8
+FP8X4 = mybir.dt.float8_e4m3fn_x4
+FP4X4 = mybir.dt.float4_e2m1fn_x4
+ACT = mybir.ActivationFunctionType
+ALU = mybir.AluOpType
+
+P = 128
+PACK = 4
+KP = P * PACK
+T = 2048
+S = 512
+H = 1024
+T2 = 1024
+S2 = 1024
+J = 512
+BANK = 512
+FLOPS = 2 * (1024 * H * S + H * S2 * T2)
+
+
+def tile_list_eclipse_phase_scorer_kernel(
+    tc, tab_words, tab_scales, offs, w1, w4_words, w4_scales, b1, gain, page0, wgs, offs3,
+    tab2_words, tab2_scales, offs2, pos1, pos2, vis, out,
+):
+    nc = tc.nc
+    with ExitStack() as ctx:
+        sb = ctx.enter_context(tc.tile_pool(name="sb", bufs=1))
+        ps = ctx.enter_context(tc.psum_pool(name="ps", bufs=1))
+
+        def tile(shape, dtype, name, tag=None):
+            return sb.tile(shape, dtype, name=name, tag=tag or name, align_bytes=64)
+
+        def bank(i, name):
+            return ps.tile([P, BANK], F32, name=name, tag="bank%d" % (i % 8))
+
+        def load_list(src, name):
+            t = sb.tile([P, src.shape[1]], U16, name=name)
+            nc.sync.dma_start(t[:], src)
+            return t
+
+        def load_words(src, name):
+            t = tile([P, T], I32, name)
+            nc.sync.dma_start(t[:], src.rearrange("p t i -> p (t i)").bitcast(I32))
+            return t
+
+        def load_scale_rows(queues, dst, first, src):
+            for q in range(4):
+                queues[q].dma_start(
+                    dst[32 * q + first : 32 * q + first + 4, :].bitcast(I32),
+                    src[4 * q : 4 * q + 4, :].bitcast(I32),
+                )
+
+        w4s_raw = tile([P, H], U8, "w4s_raw")
+        ts = tile([P, T], U8, "ts")
+        ts2 = tile([P, T], U8, "ts2")
+        nc.gpsimd.memset(ts[:].bitcast(I32), 0)
+        nc.vector.memset(ts2[:].bitcast(I32), 0)
+
+        w1_rows = w1.rearrange("(p j) c -> p j c", j=PACK)
+        page_rows = page0.rearrange("(b p t) n -> b t p n", b=2, t=PACK)
+
+        offs_t = load_list(offs, "offs_t")
+        w4w_raw = tile([P, 2 * H], U8, "w4w_raw")
+        nc.sync.dma_start(w4w_raw[:].bitcast(I32), w4_words[0].bitcast(I32))
+        for q in range(4):
+            nc.sync.dma_start(
+                w4s_raw[32 * q : 32 * q + 32, :].bitcast(I32),
+                w4_scales[0, 4 * q : 4 * q + 4, :].bitcast(I32).unsqueeze(0).broadcast_to([8, 4, H // 4]),
+            )
+        b1_t = tile([P, 2, PACK], F32, "b1_t")
+        nc.sync.dma_start(b1_t[:], b1.rearrange("(b p t) -> p b t", b=2, t=PACK))
+        w1_raw = [tile([P, PACK, KP], F32, "w1_raw%d" % b) for b in range(2)]
+        nc.sync.dma_start(w1_raw[0][:], w1_rows[:, :, 0:KP])
+        load_scale_rows([nc.gpsimd] * 2 + [nc.sync] * 2, ts, 0, tab_scales[1])
+        load_scale_rows([nc.sync] * 4, ts, 4, tab_scales[0])
+        tw0 = load_words(tab_words[0], "tw0")
+        tw1 = load_words(tab_words[1], "tw1")
+        gain_t = tile([P, 2, PACK], F32, "gain_t")
+        nc.sync.dma_start(gain_t[:], gain.rearrange("(b p t) -> p b t", b=2, t=PACK))
+        offs3_t = load_list(offs3, "offs3_t")
+        page = [tile([P, T2], F32, "page%d" % i) for i in range(8)]
+        nc.sync.dma_start(page[0][:], page_rows[0, 0])
+        wg = tile([P, PACK * S], F32, "wg")
+        for q in (0, 2, 1, 3):
+            nc.sync.dma_start(wg[32 * q : 32 * q + 32, :], wgs.rearrange("(q t) j -> q (t j)", t=PACK))
+        nc.sync.dma_start(w1_raw[1][:], w1_rows[:, :, KP : 2 * KP])
+        for i in range(1, 8):
+            nc.sync.dma_start(page[i][:], page_rows[i // PACK, i % PACK])
+        offs2_t = load_list(offs2, "offs2_t")
+        for q in range(4):
+            nc.sync.dma_start(
+                ts2[32 * q : 32 * q + 8, :].bitcast(I32), tab2_scales[:, 4 * q : 4 * q + 4, :].bitcast(I32)
+            )
+        t2w = [load_words(tab2_words[a], "t2w%d" % a) for a in range(2)]
+        pos1_t = load_list(pos1, "pos1_t")
+        pos2_t = load_list(pos2, "pos2_t")
+        vis_t = [tile([P, J], F32, "vis%d" % m) for m in range(8)]
+        for m in range(8):
+            nc.sync.dma_start(vis_t[m][:], vis[P * m : P * (m + 1), :])
+
+        w4w = tile([P, 2 * H], U8, "w4w")
+        nc.vector.tensor_copy(
+            w4w[:].rearrange("p (b t q e) -> p b t q e", b=2, t=PACK, e=2),
+            w4w_raw[:].rearrange("p (b q t e) -> p b t q e", b=2, t=PACK, e=2),
+        )
+        w4s = tile([P, H], U8, "w4s")
+        nc.vector.tensor_copy(
+            w4s[:].rearrange("p (b t q) -> p b t q", b=2, t=PACK),
+            w4s_raw[:].rearrange("p (b q t) -> p b t q", b=2, t=PACK),
+        )
+
+        def round_w1(b):
+            wb = tile([P, PACK * KP], BF16, "w1_bf%d" % b)
+            nc.scalar.copy(
+                wb[:].rearrange("p (t m j) -> p m t j", t=PACK, j=PACK),
+                w1_raw[b][:].rearrange("p j (m t) -> p m t j", t=PACK),
+            )
+            return wb
+
+        def quantise(src, width, name, tag):
+            codes = tile([P, width], U32, name + "_codes", tag)
+            plane = tile([P, width], U8, name + "_plane")
+            nc.vector.quantize_mx(codes[:].bitcast(FP8X4), plane[:], src)
+            return codes, plane
+
+        w1q = [quantise(round_w1(0)[:], KP, "w1q0", None)]
+
+        vw = tile([P, 2, S], U32, "vw")
+        vs = tile([P, S], U8, "vs")
+        nc.vector.tensor_copy(vs[:], ts[:].indirect(offs_t[:]))
+        nc.vector.tensor_copy(vw[:, 0, :], tw0[:].bitcast(U32).indirect(offs_t[:]))
+        nc.vector.tensor_copy(vw[:, 1, :], tw1[:].bitcast(U32).indirect(offs_t[:]))
+
+        def features(i):
+            b, t = divmod(i, PACK)
+            x = bank(i, "x%d" % i)
+            codes, plane = w1q[b]
+            nc.tensor.matmul_mx(
+                x[:], lhsT=codes[:, P * t : P * (t + 1)].bitcast(FP8X4), lhsT_scale=plane[:, P * t : P * (t + 1)],
+                rhs=vw[:, 0, :].bitcast(FP8X4), rhs_scale=vs[4:P, :], start=True, stop=False,
+            )
+            nc.tensor.matmul_mx(
+                x[:], lhsT=w4w[:, 2 * P * i : 2 * P * (i + 1)].bitcast(FP4X4), lhsT_scale=w4s[:, P * i : P * (i + 1)],
+                rhs=vw[:, 1, :].bitcast(FP8X4), rhs_scale=vs[:], start=False, stop=True,
+            )
+            s = tile([P, S], F32, "sin%d" % i, "sin%d" % (i % 2))
+            nc.scalar.activation(s[:], x[:], ACT.Sin, bias=b1_t[:, b, t : t + 1])
+            h = tile([P, S], F32, "h%d" % i)
+            nc.scalar.activation(h[:], s[:], ACT.Copy, scale=gain_t[:, b, t : t + 1])
+            return h
+
+        def scatter(i, h):
+            t = i % PACK
+            nc.vector.tensor_tensor(page[i][:].indirect(offs3_t[:]), h[:], wg[:, S * t : S * (t + 1)], ALU.mult)
+
+        hs = [features(i) for i in range(PACK)]
+        wb1 = round_w1(1)
+        scatter(0, hs[0])
+        scatter(1, hs[1])
+        w1q.append(quantise(wb1[:], KP, "w1q1", "h1"))
+        hs = hs + [features(i) for i in range(PACK, 8)]
+        for i in range(2, 8):
+            scatter(i, hs[i])
+
+        def round_pairs(a):
+            pairs = tile([P, 2, T2, 2], BF16, "pairs%d" % a, "w1_raw%d" % (1 - a))
+            for t in range(PACK):
+                nc.scalar.copy(pairs[:, t // 2, :, t % 2], page[PACK * a + t][:])
+            return pairs[:].rearrange("p u n e -> p (u n e)").bitcast(U32).rearrange("p (u n) -> p n u", u=2)
+
+        def weave(words, n0, width, name):
+            woven = tile([P, PACK * width], BF16, name)
+            nc.scalar.copy(woven[:].bitcast(U32).rearrange("p (n u) -> p n u", u=2), words[:, n0 : n0 + width, :])
+            return woven
+
+        pq0 = quantise(weave(round_pairs(0), 0, T2, "woven0")[:], T2, "pq0", "h6")
+
+        def gather_candidates(g, words_tag, plane_tag):
+            cw = tile([P, 2, S], U32, "cw%d" % g, words_tag)
+            cs = tile([P, S], U8, "cs%d" % g, plane_tag)
+            part = offs2_t[:, 32 * g : 32 * (g + 1)]
+            nc.vector.tensor_copy(cs[:], ts2[:].indirect(part))
+            for a in range(2):
+                nc.vector.tensor_copy(cw[:, a, :], t2w[a][:].bitcast(U32).indirect(part))
+            return cw, cs
+
+        cand = [gather_candidates(0, "wg", "h7")]
+        words1 = round_pairs(1)
+        pq1 = [
+            quantise(weave(words1, BANK * c, BANK, "woven1_%d" % c)[:], BANK, "pq1_%d" % c, "h%d" % (2 * c))
+            for c in range(2)
+        ]
+        cand.append(gather_candidates(1, "woven1_1", "woven1_0"))
+
+        for m in range(8):
+            cw, cs = cand[m // 4]
+            cols = slice(P * (m % 4), P * (m % 4 + 1))
+            e = tile([P, T2], F32, "e%d" % m, "e%d" % (m % 3))
+            for c in range(2):
+                acc = bank(2 * m + c, "acc%d_%d" % (m, c))
+                n = slice(BANK * c, BANK * (c + 1))
+                nc.tensor.matmul_mx(
+                    acc[:], lhsT=cw[:, 0, cols].bitcast(FP8X4), lhsT_scale=cs[:, cols],
+                    rhs=pq0[0][:, n].bitcast(FP8X4), rhs_scale=pq0[1][:, n], start=True, stop=False,
+                )
+                nc.tensor.matmul_mx(
+                    acc[:], lhsT=cw[:, 1, cols].bitcast(FP8X4), lhsT_scale=cs[4:P, cols],
+                    rhs=pq1[c][0][:].bitcast(FP8X4), rhs_scale=pq1[c][1][:], start=False, stop=True,
+                )
+                nc.scalar.copy(e[:, n], acc[:])
+            first = tile([P, J], F32, "first%d" % m, "first%d" % (m % 2))
+            second = tile([P, J], F32, "second%d" % m, "second%d" % (m % 2))
+            nc.vector.tensor_copy(first[:], e[:].indirect(pos1_t[:]))
+            nc.vector.tensor_copy(second[:], e[:].indirect(pos2_t[:]))
+            deeper = tile([P, J], F32, "deeper%d" % m, "deeper%d" % (m % 2))
+            nc.vector.tensor_tensor(deeper[:], first[:], second[:], ALU.max)
+            res = tile([P, J], F32, "res%d" % m, "res%d" % (m % 3))
+            nc.vector.tensor_tensor(res[:], deeper[:], vis_t[m][:], ALU.mult)
+            nc.sync.dma_start(out[P * m : P * (m + 1), :], res[:])

@@ -52,17 +52,17 @@ def tile_list_eclipse_phase_scorer_kernel(
             return t
 
         def load_scale_rows(queues, dst, first, src):
-            for q in range(4):
-                queues[q].dma_start(
-                    dst[32 * q + first : 32 * q + first + 4, :].bitcast(I32),
-                    src[4 * q : 4 * q + 4, :].bitcast(I32),
-                )
+            for r in range(4):
+                queues[r].dma_start(dst[first + r : P : 32, :].bitcast(I32), src[r:16:4, :].bitcast(I32))
 
         w4s_raw = tile([P, H], U8, "w4s_raw")
         ts = tile([P, T], U8, "ts")
         ts2 = tile([P, T], U8, "ts2")
         nc.gpsimd.memset(ts[:].bitcast(I32), 0)
         nc.vector.memset(ts2[:].bitcast(I32), 0)
+        warm = tile([P, 2], F32, "warm")
+        nc.vector.memset(warm[:, 0:1], 0.0)
+        nc.scalar.activation(warm[:, 1:2], warm[:, 0:1], ACT.Sin)
 
         w1_rows = w1.rearrange("(p j) c -> p j c", j=PACK)
         page_rows = page0.rearrange("(b p t) n -> b t p n", b=2, t=PACK)
@@ -75,24 +75,29 @@ def tile_list_eclipse_phase_scorer_kernel(
                 w4s_raw[32 * q : 32 * q + 32, :].bitcast(I32),
                 w4_scales[0, 4 * q : 4 * q + 4, :].bitcast(I32).unsqueeze(0).broadcast_to([8, 4, H // 4]),
             )
-        b1_t = tile([P, 2, PACK], F32, "b1_t")
-        nc.sync.dma_start(b1_t[:], b1.rearrange("(b p t) -> p b t", b=2, t=PACK))
         w1_raw = [tile([P, PACK, KP], F32, "w1_raw%d" % b) for b in range(2)]
         nc.sync.dma_start(w1_raw[0][:], w1_rows[:, :, 0:KP])
-        load_scale_rows([nc.gpsimd] * 2 + [nc.sync] * 2, ts, 0, tab_scales[1])
-        load_scale_rows([nc.sync] * 4, ts, 4, tab_scales[0])
         tw0 = load_words(tab_words[0], "tw0")
-        tw1 = load_words(tab_words[1], "tw1")
+        load_scale_rows([nc.gpsimd] * 3 + [nc.sync], ts, 0, tab_scales[1])
+        load_scale_rows([nc.sync] * 4, ts, 4, tab_scales[0])
+        b1_t = tile([P, 2, PACK], F32, "b1_t")
+        nc.gpsimd.dma_start(b1_t[:], b1.rearrange("(b p t) -> p b t", b=2, t=PACK))
         gain_t = tile([P, 2, PACK], F32, "gain_t")
-        nc.sync.dma_start(gain_t[:], gain.rearrange("(b p t) -> p b t", b=2, t=PACK))
+        nc.gpsimd.dma_start(gain_t[:], gain.rearrange("(b p t) -> p b t", b=2, t=PACK))
+        tw1 = load_words(tab_words[1], "tw1")
         offs3_t = load_list(offs3, "offs3_t")
         page = [tile([P, T2], F32, "page%d" % i) for i in range(8)]
         nc.sync.dma_start(page[0][:], page_rows[0, 0])
-        wg = tile([P, PACK * S], F32, "wg")
-        for q in (0, 2, 1, 3):
-            nc.sync.dma_start(wg[32 * q : 32 * q + 32, :], wgs.rearrange("(q t) j -> q (t j)", t=PACK))
+        wgs_rows = wgs.rearrange("(q t) j -> q (t j)", t=PACK)
+        wg_first = tile([P, S], F32, "wg_first")
+        wg_rest = tile([P, (PACK - 1) * S], F32, "wg")
+        for part, src in ((wg_first, wgs_rows[:, 0:S]), (wg_rest, wgs_rows[:, S : PACK * S])):
+            for q in (0, 2, 1, 3):
+                nc.sync.dma_start(part[32 * q : 32 * q + 32, :], src)
+        wg = [wg_first[:]] + [wg_rest[:, S * t : S * (t + 1)] for t in range(PACK - 1)]
+        nc.sync.dma_start(page[1][:], page_rows[0, 1])
         nc.sync.dma_start(w1_raw[1][:], w1_rows[:, :, KP : 2 * KP])
-        for i in range(1, 8):
+        for i in range(2, 8):
             nc.sync.dma_start(page[i][:], page_rows[i // PACK, i % PACK])
         offs2_t = load_list(offs2, "offs2_t")
         for q in range(4):
@@ -135,40 +140,52 @@ def tile_list_eclipse_phase_scorer_kernel(
 
         vw = tile([P, 2, S], U32, "vw")
         vs = tile([P, S], U8, "vs")
-        nc.vector.tensor_copy(vs[:], ts[:].indirect(offs_t[:]))
         nc.vector.tensor_copy(vw[:, 0, :], tw0[:].bitcast(U32).indirect(offs_t[:]))
-        nc.vector.tensor_copy(vw[:, 1, :], tw1[:].bitcast(U32).indirect(offs_t[:]))
+        nc.vector.tensor_copy(vs[:], ts[:].indirect(offs_t[:]))
+        halves = [slice(0, S // 2), slice(S // 2, S)]
 
-        def features(i):
+        def entries(lst, js):
+            return lst[:, js.start // 16 : js.stop // 16]
+
+        for js in halves:
+            nc.vector.tensor_copy(vw[:, 1, js], tw1[:].bitcast(U32).indirect(entries(offs_t, js)))
+
+        def features(i, h, js, bank_no, sin_tag):
             b, t = divmod(i, PACK)
-            x = bank(i, "x%d" % i)
+            x = bank(bank_no, "x%d_%d" % (i, js.start))[:, 0 : js.stop - js.start]
             codes, plane = w1q[b]
             nc.tensor.matmul_mx(
-                x[:], lhsT=codes[:, P * t : P * (t + 1)].bitcast(FP8X4), lhsT_scale=plane[:, P * t : P * (t + 1)],
-                rhs=vw[:, 0, :].bitcast(FP8X4), rhs_scale=vs[4:P, :], start=True, stop=False,
+                x, lhsT=w4w[:, 2 * P * i : 2 * P * (i + 1)].bitcast(FP4X4), lhsT_scale=w4s[:, P * i : P * (i + 1)],
+                rhs=vw[:, 1, js].bitcast(FP8X4), rhs_scale=vs[:, js], start=True, stop=False,
             )
             nc.tensor.matmul_mx(
-                x[:], lhsT=w4w[:, 2 * P * i : 2 * P * (i + 1)].bitcast(FP4X4), lhsT_scale=w4s[:, P * i : P * (i + 1)],
-                rhs=vw[:, 1, :].bitcast(FP8X4), rhs_scale=vs[:], start=False, stop=True,
+                x, lhsT=codes[:, P * t : P * (t + 1)].bitcast(FP8X4), lhsT_scale=plane[:, P * t : P * (t + 1)],
+                rhs=vw[:, 0, js].bitcast(FP8X4), rhs_scale=vs[4:P, js], start=False, stop=True,
             )
-            s = tile([P, S], F32, "sin%d" % i, "sin%d" % (i % 2))
-            nc.scalar.activation(s[:], x[:], ACT.Sin, bias=b1_t[:, b, t : t + 1])
-            h = tile([P, S], F32, "h%d" % i)
-            nc.scalar.activation(h[:], s[:], ACT.Copy, scale=gain_t[:, b, t : t + 1])
-            return h
+            s = tile([P, js.stop - js.start], F32, "sin%d_%d" % (i, js.start), sin_tag)
+            nc.scalar.activation(s[:], x, ACT.Sin, bias=b1_t[:, b, t : t + 1])
+            nc.scalar.activation(h[:, js], s[:], ACT.Copy, scale=gain_t[:, b, t : t + 1])
 
-        def scatter(i, h):
-            t = i % PACK
-            nc.vector.tensor_tensor(page[i][:].indirect(offs3_t[:]), h[:], wg[:, S * t : S * (t + 1)], ALU.mult)
+        def scatter(i, js):
+            nc.vector.tensor_tensor(page[i][:].indirect(entries(offs3_t, js)), hs[i][:, js], wg[i % PACK][:, js], ALU.mult)
 
-        hs = [features(i) for i in range(PACK)]
+        whole = slice(0, S)
+        hs = [tile([P, S], F32, "h%d" % i) for i in range(8)]
+        features(0, hs[0], halves[0], 0, "sin0")
+        features(0, hs[0], halves[1], 7, "sin1")
+        features(1, hs[1], whole, 1, "sin0")
+        features(2, hs[2], whole, 2, "sin1")
         wb1 = round_w1(1)
-        scatter(0, hs[0])
-        scatter(1, hs[1])
-        w1q.append(quantise(wb1[:], KP, "w1q1", "h1"))
-        hs = hs + [features(i) for i in range(PACK, 8)]
-        for i in range(2, 8):
-            scatter(i, hs[i])
+        features(3, hs[3], whole, 3, "w1_raw1")
+        for js in halves:
+            scatter(0, js)
+        scatter(1, whole)
+        scatter(2, whole)
+        w1q.append(quantise(wb1[:], KP, "w1q1", "h2"))
+        for i in range(PACK, 8):
+            features(i, hs[i], whole, i, "sin%d" % (i % 2))
+        for i in range(3, 8):
+            scatter(i, whole)
 
         def round_pairs(a):
             pairs = tile([P, 2, T2, 2], BF16, "pairs%d" % a, "w1_raw%d" % (1 - a))
@@ -223,5 +240,6 @@ def tile_list_eclipse_phase_scorer_kernel(
             deeper = tile([P, J], F32, "deeper%d" % m, "deeper%d" % (m % 2))
             nc.vector.tensor_tensor(deeper[:], first[:], second[:], ALU.max)
             res = tile([P, J], F32, "res%d" % m, "res%d" % (m % 3))
-            nc.vector.tensor_tensor(res[:], deeper[:], vis_t[m][:], ALU.mult)
+            weigher = nc.vector if m == 7 else nc.gpsimd
+            weigher.tensor_tensor(res[:], deeper[:], vis_t[m][:], ALU.mult)
             nc.sync.dma_start(out[P * m : P * (m + 1), :], res[:])

@@ -80,30 +80,35 @@ def tile_list_eclipse_phase_scorer_kernel(
         tw0 = load_words(tab_words[0], "tw0")
         load_scale_rows([nc.gpsimd] * 3 + [nc.sync], ts, 0, tab_scales[1])
         load_scale_rows([nc.sync] * 4, ts, 4, tab_scales[0])
-        b1_t = tile([P, 2, PACK], F32, "b1_t")
-        nc.gpsimd.dma_start(b1_t[:], b1.rearrange("(b p t) -> p b t", b=2, t=PACK))
-        gain_t = tile([P, 2, PACK], F32, "gain_t")
-        nc.gpsimd.dma_start(gain_t[:], gain.rearrange("(b p t) -> p b t", b=2, t=PACK))
+        for q in range(4):
+            nc.gpsimd.dma_start(
+                ts2[32 * q : 32 * q + 8, :].bitcast(I32), tab2_scales[:, 4 * q : 4 * q + 4, :].bitcast(I32)
+            )
         tw1 = load_words(tab_words[1], "tw1")
+        b1_t = tile([P, 2, PACK], F32, "b1_t")
+        nc.sync.dma_start(b1_t[:], b1.rearrange("(b p t) -> p b t", b=2, t=PACK))
+        gain_t = tile([P, 2, PACK], F32, "gain_t")
+        nc.sync.dma_start(gain_t[:], gain.rearrange("(b p t) -> p b t", b=2, t=PACK))
+        offs2_t = load_list(offs2, "offs2_t")
         offs3_t = load_list(offs3, "offs3_t")
         page = [tile([P, T2], F32, "page%d" % i) for i in range(8)]
         nc.sync.dma_start(page[0][:], page_rows[0, 0])
         wgs_rows = wgs.rearrange("(q t) j -> q (t j)", t=PACK)
-        wg_first = tile([P, S], F32, "wg_first")
-        wg_rest = tile([P, (PACK - 1) * S], F32, "wg")
-        for part, src in ((wg_first, wgs_rows[:, 0:S]), (wg_rest, wgs_rows[:, S : PACK * S])):
+
+        def load_wgs(t0, t1):
+            part = tile([P, (t1 - t0) * S], F32, "wg%d" % t0)
             for q in (0, 2, 1, 3):
-                nc.sync.dma_start(part[32 * q : 32 * q + 32, :], src)
-        wg = [wg_first[:]] + [wg_rest[:, S * t : S * (t + 1)] for t in range(PACK - 1)]
+                nc.sync.dma_start(part[32 * q : 32 * q + 32, :], wgs_rows[:, S * t0 : S * t1])
+            return [part[:, S * t : S * (t + 1)] for t in range(t1 - t0)]
+
+        wg = load_wgs(0, 1)
         nc.sync.dma_start(page[1][:], page_rows[0, 1])
+        wg = wg + load_wgs(1, 2)
         nc.sync.dma_start(w1_raw[1][:], w1_rows[:, :, KP : 2 * KP])
-        for i in range(2, 8):
+        nc.sync.dma_start(page[2][:], page_rows[0, 2])
+        wg = wg + load_wgs(2, PACK)
+        for i in range(3, 8):
             nc.sync.dma_start(page[i][:], page_rows[i // PACK, i % PACK])
-        offs2_t = load_list(offs2, "offs2_t")
-        for q in range(4):
-            nc.sync.dma_start(
-                ts2[32 * q : 32 * q + 8, :].bitcast(I32), tab2_scales[:, 4 * q : 4 * q + 4, :].bitcast(I32)
-            )
         t2w = [load_words(tab2_words[a], "t2w%d" % a) for a in range(2)]
         pos1_t = load_list(pos1, "pos1_t")
         pos2_t = load_list(pos2, "pos2_t")
@@ -150,24 +155,40 @@ def tile_list_eclipse_phase_scorer_kernel(
         for js in halves:
             nc.vector.tensor_copy(vw[:, 1, js], tw1[:].bitcast(U32).indirect(entries(offs_t, js)))
 
-        def features(i, h, js, bank_no, sin_tag):
+        def gather_candidate_plane(g, tag):
+            cs = tile([P, S], U8, "cs%d" % g, tag)
+            nc.vector.tensor_copy(cs[:], ts2[:].indirect(offs2_t[:, 32 * g : 32 * (g + 1)]))
+            return cs
+
+        planes = [gather_candidate_plane(0, None)]
+
+        def features(i, put, js, bank_no, sin_tag):
             b, t = divmod(i, PACK)
             x = bank(bank_no, "x%d_%d" % (i, js.start))[:, 0 : js.stop - js.start]
             codes, plane = w1q[b]
-            nc.tensor.matmul_mx(
-                x, lhsT=w4w[:, 2 * P * i : 2 * P * (i + 1)].bitcast(FP4X4), lhsT_scale=w4s[:, P * i : P * (i + 1)],
-                rhs=vw[:, 1, js].bitcast(FP8X4), rhs_scale=vs[:, js], start=True, stop=False,
-            )
-            nc.tensor.matmul_mx(
-                x, lhsT=codes[:, P * t : P * (t + 1)].bitcast(FP8X4), lhsT_scale=plane[:, P * t : P * (t + 1)],
-                rhs=vw[:, 0, js].bitcast(FP8X4), rhs_scale=vs[4:P, js], start=False, stop=True,
-            )
+            passes = [
+                (w4w[:, 2 * P * i : 2 * P * (i + 1)].bitcast(FP4X4), w4s[:, P * i : P * (i + 1)], vw[:, 1, js], vs[:, js]),
+                (codes[:, P * t : P * (t + 1)].bitcast(FP8X4), plane[:, P * t : P * (t + 1)], vw[:, 0, js], vs[4:P, js]),
+            ]
+            if i == 0 and js.start == 0:
+                passes = passes[::-1]
+            for n, (w_codes, w_plane, v_words, v_plane) in enumerate(passes):
+                nc.tensor.matmul_mx(
+                    x, lhsT=w_codes, lhsT_scale=w_plane, rhs=v_words.bitcast(FP8X4), rhs_scale=v_plane,
+                    start=n == 0, stop=n == 1,
+                )
             s = tile([P, js.stop - js.start], F32, "sin%d_%d" % (i, js.start), sin_tag)
             nc.scalar.activation(s[:], x, ACT.Sin, bias=b1_t[:, b, t : t + 1])
-            nc.scalar.activation(h[:, js], s[:], ACT.Copy, scale=gain_t[:, b, t : t + 1])
+            h = tile([P, js.stop - js.start], F32, "h%d_%d" % (i, js.start), "h_%d" % (bank_no % 2))
+            if i <= 1:
+                nc.scalar.activation(h[:], s[:], ACT.Copy, scale=gain_t[:, b, t : t + 1])
+            else:
+                nc.gpsimd.tensor_scalar(h[:], s[:], gain_t[:, b, t : t + 1], 0.0, ALU.mult, ALU.add)
+            weigher = nc.vector if i == 0 and js.start == 0 else nc.gpsimd
+            weigher.tensor_tensor(put[:, js], h[:], wg[t][:, js], ALU.mult)
 
         def scatter(i, js):
-            nc.vector.tensor_tensor(page[i][:].indirect(entries(offs3_t, js)), hs[i][:, js], wg[i % PACK][:, js], ALU.mult)
+            nc.vector.tensor_copy(page[i][:].indirect(entries(offs3_t, js)), hs[i][:, js])
 
         whole = slice(0, S)
         hs = [tile([P, S], F32, "h%d" % i) for i in range(8)]
@@ -175,16 +196,15 @@ def tile_list_eclipse_phase_scorer_kernel(
         features(0, hs[0], halves[1], 7, "sin1")
         features(1, hs[1], whole, 1, "sin0")
         features(2, hs[2], whole, 2, "sin1")
+        features(3, hs[3], whole, 3, "sin0")
         wb1 = round_w1(1)
-        features(3, hs[3], whole, 3, "w1_raw1")
         for js in halves:
             scatter(0, js)
         scatter(1, whole)
-        scatter(2, whole)
-        w1q.append(quantise(wb1[:], KP, "w1q1", "h2"))
+        w1q.append(quantise(wb1[:], KP, "w1q1", "h1"))
         for i in range(PACK, 8):
-            features(i, hs[i], whole, i, "sin%d" % (i % 2))
-        for i in range(3, 8):
+            features(i, hs[i], whole, i, "sin%d" % ((i + 1) % 2))
+        for i in range(2, 8):
             scatter(i, whole)
 
         def round_pairs(a):
@@ -200,37 +220,35 @@ def tile_list_eclipse_phase_scorer_kernel(
 
         pq0 = quantise(weave(round_pairs(0), 0, T2, "woven0")[:], T2, "pq0", "h6")
 
-        def gather_candidates(g, words_tag, plane_tag):
-            cw = tile([P, 2, S], U32, "cw%d" % g, words_tag)
-            cs = tile([P, S], U8, "cs%d" % g, plane_tag)
-            part = offs2_t[:, 32 * g : 32 * (g + 1)]
-            nc.vector.tensor_copy(cs[:], ts2[:].indirect(part))
+        def gather_candidates(g, tag):
+            cw = tile([P, 2, S], U32, "cw%d" % g, tag)
             for a in range(2):
-                nc.vector.tensor_copy(cw[:, a, :], t2w[a][:].bitcast(U32).indirect(part))
-            return cw, cs
+                nc.vector.tensor_copy(cw[:, a, :], t2w[a][:].bitcast(U32).indirect(offs2_t[:, 32 * g : 32 * (g + 1)]))
+            return cw
 
-        cand = [gather_candidates(0, "wg", "h7")]
+        cand = [gather_candidates(0, "h7")]
         words1 = round_pairs(1)
         pq1 = [
             quantise(weave(words1, BANK * c, BANK, "woven1_%d" % c)[:], BANK, "pq1_%d" % c, "h%d" % (2 * c))
             for c in range(2)
         ]
-        cand.append(gather_candidates(1, "woven1_1", "woven1_0"))
+        planes.append(gather_candidate_plane(1, "woven1_0"))
+        cand.append(gather_candidates(1, "woven1_1"))
 
         for m in range(8):
-            cw, cs = cand[m // 4]
+            cw, cs = cand[m // 4], planes[m // 4]
             cols = slice(P * (m % 4), P * (m % 4 + 1))
             e = tile([P, T2], F32, "e%d" % m, "e%d" % (m % 3))
             for c in range(2):
                 acc = bank(2 * m + c, "acc%d_%d" % (m, c))
                 n = slice(BANK * c, BANK * (c + 1))
                 nc.tensor.matmul_mx(
-                    acc[:], lhsT=cw[:, 0, cols].bitcast(FP8X4), lhsT_scale=cs[:, cols],
-                    rhs=pq0[0][:, n].bitcast(FP8X4), rhs_scale=pq0[1][:, n], start=True, stop=False,
+                    acc[:], lhsT=cw[:, 1, cols].bitcast(FP8X4), lhsT_scale=cs[4:P, cols],
+                    rhs=pq1[c][0][:].bitcast(FP8X4), rhs_scale=pq1[c][1][:], start=True, stop=False,
                 )
                 nc.tensor.matmul_mx(
-                    acc[:], lhsT=cw[:, 1, cols].bitcast(FP8X4), lhsT_scale=cs[4:P, cols],
-                    rhs=pq1[c][0][:].bitcast(FP8X4), rhs_scale=pq1[c][1][:], start=False, stop=True,
+                    acc[:], lhsT=cw[:, 0, cols].bitcast(FP8X4), lhsT_scale=cs[:, cols],
+                    rhs=pq0[0][:, n].bitcast(FP8X4), rhs_scale=pq0[1][:, n], start=False, stop=True,
                 )
                 nc.scalar.copy(e[:, n], acc[:])
             first = tile([P, J], F32, "first%d" % m, "first%d" % (m % 2))

@@ -1,6 +1,7 @@
 from contextlib import ExitStack
 
 import concourse.mybir as mybir
+from concourse.masks import make_identity
 
 F32 = mybir.dt.float32
 BF16 = mybir.dt.bfloat16
@@ -58,6 +59,8 @@ def tile_list_eclipse_phase_scorer_kernel(
         w4s_raw = tile([P, H], U8, "w4s_raw")
         ts = tile([P, T], U8, "ts")
         ts2 = tile([P, T], U8, "ts2")
+        identity = tile([P, P], F32, "identity")
+        make_identity(nc, identity[:])
         nc.gpsimd.memset(ts[:].bitcast(I32), 0)
         nc.vector.memset(ts2[:].bitcast(I32), 0)
         warm = tile([P, 2], F32, "warm")
@@ -68,6 +71,8 @@ def tile_list_eclipse_phase_scorer_kernel(
         page_rows = page0.rearrange("(b p t) n -> b t p n", b=2, t=PACK)
 
         offs_t = load_list(offs, "offs_t")
+        wgs_raw = tile([P, S], F32, "wgs_raw")
+        nc.sync.dma_start(wgs_raw[:], wgs)
         w4w_raw = tile([P, 2 * H], U8, "w4w_raw")
         nc.sync.dma_start(w4w_raw[:].bitcast(I32), w4_words[0].bitcast(I32))
         for q in range(4):
@@ -80,41 +85,43 @@ def tile_list_eclipse_phase_scorer_kernel(
         tw0 = load_words(tab_words[0], "tw0")
         load_scale_rows([nc.gpsimd] * 3 + [nc.sync], ts, 0, tab_scales[1])
         load_scale_rows([nc.sync] * 4, ts, 4, tab_scales[0])
-        for q in range(4):
-            nc.gpsimd.dma_start(
-                ts2[32 * q : 32 * q + 8, :].bitcast(I32), tab2_scales[:, 4 * q : 4 * q + 4, :].bitcast(I32)
-            )
         tw1 = load_words(tab_words[1], "tw1")
         b1_t = tile([P, 2, PACK], F32, "b1_t")
         nc.sync.dma_start(b1_t[:], b1.rearrange("(b p t) -> p b t", b=2, t=PACK))
         gain_t = tile([P, 2, PACK], F32, "gain_t")
         nc.sync.dma_start(gain_t[:], gain.rearrange("(b p t) -> p b t", b=2, t=PACK))
-        offs2_t = load_list(offs2, "offs2_t")
         offs3_t = load_list(offs3, "offs3_t")
         page = [tile([P, T2], F32, "page%d" % i) for i in range(8)]
-        nc.sync.dma_start(page[0][:], page_rows[0, 0])
-        wgs_rows = wgs.rearrange("(q t) j -> q (t j)", t=PACK)
-
-        def load_wgs(t0, t1):
-            part = tile([P, (t1 - t0) * S], F32, "wg%d" % t0)
-            for q in (0, 2, 1, 3):
-                nc.sync.dma_start(part[32 * q : 32 * q + 32, :], wgs_rows[:, S * t0 : S * t1])
-            return [part[:, S * t : S * (t + 1)] for t in range(t1 - t0)]
-
-        wg = load_wgs(0, 1)
-        nc.sync.dma_start(page[1][:], page_rows[0, 1])
-        wg = wg + load_wgs(1, 2)
-        nc.sync.dma_start(w1_raw[1][:], w1_rows[:, :, KP : 2 * KP])
-        nc.sync.dma_start(page[2][:], page_rows[0, 2])
-        wg = wg + load_wgs(2, PACK)
-        for i in range(3, 8):
+        for i in range(8):
+            if i == 1:
+                nc.sync.dma_start(w1_raw[1][:], w1_rows[:, :, KP : 2 * KP])
             nc.sync.dma_start(page[i][:], page_rows[i // PACK, i % PACK])
+        offs2_t = load_list(offs2, "offs2_t")
+        for q in range(4):
+            nc.sync.dma_start(
+                ts2[32 * q : 32 * q + 8, :].bitcast(I32), tab2_scales[:, 4 * q : 4 * q + 4, :].bitcast(I32)
+            )
         t2w = [load_words(tab2_words[a], "t2w%d" % a) for a in range(2)]
         pos1_t = load_list(pos1, "pos1_t")
         pos2_t = load_list(pos2, "pos2_t")
         vis_t = [tile([P, J], F32, "vis%d" % m) for m in range(8)]
         for m in range(8):
             nc.sync.dma_start(vis_t[m][:], vis[P * m : P * (m + 1), :])
+
+        turned = bank(2, "wgs_turned")
+        for jb in range(4):
+            nc.tensor.transpose(turned[:, P * jb : P * (jb + 1)], wgs_raw[:, P * jb : P * (jb + 1)], identity[:])
+        dealt = tile([P, 4, PACK, P], F32, "wgs_dealt")
+        nc.vector.tensor_copy(
+            dealt[:].rearrange("j b t (r q) -> j b t r q", r=4),
+            turned[:].rearrange("j (b q t) -> j b t q", b=4, t=PACK).unsqueeze(3).broadcast_to([P, 4, PACK, 4, 32]),
+        )
+        backs = []
+        for t in range(PACK):
+            back = bank(3 + t, "wgs_back%d" % t)
+            for jb in range(4):
+                nc.tensor.transpose(back[:, P * jb : P * (jb + 1)], dealt[:, jb, t, :], identity[:])
+            backs.append(back)
 
         w4w = tile([P, 2 * H], U8, "w4w")
         nc.vector.tensor_copy(
@@ -142,6 +149,9 @@ def tile_list_eclipse_phase_scorer_kernel(
             return codes, plane
 
         w1q = [quantise(round_w1(0)[:], KP, "w1q0", None)]
+        wg = [tile([P, S], F32, "wg%d" % t) for t in range(PACK)]
+        for t in range(PACK):
+            nc.scalar.copy(wg[t][:], backs[t][:])
 
         vw = tile([P, 2, S], U32, "vw")
         vs = tile([P, S], U8, "vs")
@@ -159,8 +169,6 @@ def tile_list_eclipse_phase_scorer_kernel(
             cs = tile([P, S], U8, "cs%d" % g, tag)
             nc.vector.tensor_copy(cs[:], ts2[:].indirect(offs2_t[:, 32 * g : 32 * (g + 1)]))
             return cs
-
-        planes = [gather_candidate_plane(0, None)]
 
         def features(i, put, js, bank_no, sin_tag):
             b, t = divmod(i, PACK)
@@ -196,14 +204,14 @@ def tile_list_eclipse_phase_scorer_kernel(
         features(0, hs[0], halves[1], 7, "sin1")
         features(1, hs[1], whole, 1, "sin0")
         features(2, hs[2], whole, 2, "sin1")
-        features(3, hs[3], whole, 3, "sin0")
         wb1 = round_w1(1)
+        features(3, hs[3], whole, 3, "w1_raw1")
         for js in halves:
             scatter(0, js)
         scatter(1, whole)
         w1q.append(quantise(wb1[:], KP, "w1q1", "h1"))
         for i in range(PACK, 8):
-            features(i, hs[i], whole, i, "sin%d" % ((i + 1) % 2))
+            features(i, hs[i], whole, i, "sin%d" % (i % 2))
         for i in range(2, 8):
             scatter(i, whole)
 
@@ -226,6 +234,7 @@ def tile_list_eclipse_phase_scorer_kernel(
                 nc.vector.tensor_copy(cw[:, a, :], t2w[a][:].bitcast(U32).indirect(offs2_t[:, 32 * g : 32 * (g + 1)]))
             return cw
 
+        planes = [gather_candidate_plane(0, "h5")]
         cand = [gather_candidates(0, "h7")]
         words1 = round_pairs(1)
         pq1 = [

from contextlib import ExitStack

import concourse.mybir as mybir
from concourse.masks import make_identity

F32 = mybir.dt.float32
BF16 = mybir.dt.bfloat16
I32 = mybir.dt.int32
U32 = mybir.dt.uint32
U16 = mybir.dt.uint16
U8 = mybir.dt.uint8
FP8X4 = mybir.dt.float8_e4m3fn_x4
FP4X4 = mybir.dt.float4_e2m1fn_x4
ACT = mybir.ActivationFunctionType
ALU = mybir.AluOpType

P = 128
PACK = 4
KP = P * PACK
T = 2048
S = 512
H = 1024
T2 = 1024
S2 = 1024
J = 512
BANK = 512
FLOPS = 2 * (1024 * H * S + H * S2 * T2)


def tile_list_eclipse_phase_scorer_kernel(
    tc, tab_words, tab_scales, offs, w1, w4_words, w4_scales, b1, gain, page0, wgs, offs3,
    tab2_words, tab2_scales, offs2, pos1, pos2, vis, out,
):
    nc = tc.nc
    with ExitStack() as ctx:
        sb = ctx.enter_context(tc.tile_pool(name="sb", bufs=1))
        ps = ctx.enter_context(tc.psum_pool(name="ps", bufs=1))

        def tile(shape, dtype, name, tag=None):
            return sb.tile(shape, dtype, name=name, tag=tag or name, align_bytes=64)

        def bank(i, name):
            return ps.tile([P, BANK], F32, name=name, tag="bank%d" % (i % 8))

        def load_list(src, name):
            t = sb.tile([P, src.shape[1]], U16, name=name)
            nc.sync.dma_start(t[:], src)
            return t

        def load_words(src, name):
            t = tile([P, T], I32, name)
            nc.sync.dma_start(t[:], src.rearrange("p t i -> p (t i)").bitcast(I32))
            return t

        def load_scale_rows(queues, dst, first, src):
            for r in range(4):
                queues[r].dma_start(dst[first + r : P : 32, :].bitcast(I32), src[r:16:4, :].bitcast(I32))

        w4s_raw = tile([P, H], U8, "w4s_raw")
        ts = tile([P, T], U8, "ts")
        ts2 = tile([P, T], U8, "ts2")
        identity = tile([P, P], F32, "identity")
        make_identity(nc, identity[:])
        nc.gpsimd.memset(ts[:].bitcast(I32), 0)
        nc.vector.memset(ts2[:].bitcast(I32), 0)
        warm = tile([P, 2], F32, "warm")
        nc.vector.memset(warm[:, 0:1], 0.0)
        nc.scalar.activation(warm[:, 1:2], warm[:, 0:1], ACT.Sin)

        w1_rows = w1.rearrange("(p j) c -> p j c", j=PACK)
        page_rows = page0.rearrange("(b p t) n -> b t p n", b=2, t=PACK)

        offs_t = load_list(offs, "offs_t")
        wgs_raw = tile([P, S], F32, "wgs_raw")
        nc.sync.dma_start(wgs_raw[:], wgs)
        w4w_raw = tile([P, 2 * H], U8, "w4w_raw")
        nc.sync.dma_start(w4w_raw[:].bitcast(I32), w4_words[0].bitcast(I32))
        for q in range(4):
            nc.sync.dma_start(
                w4s_raw[32 * q : 32 * q + 32, :].bitcast(I32),
                w4_scales[0, 4 * q : 4 * q + 4, :].bitcast(I32).unsqueeze(0).broadcast_to([8, 4, H // 4]),
            )
        w1_raw = [tile([P, PACK, KP], F32, "w1_raw%d" % b) for b in range(2)]
        nc.sync.dma_start(w1_raw[0][:], w1_rows[:, :, 0:KP])
        tw0 = load_words(tab_words[0], "tw0")
        load_scale_rows([nc.gpsimd] * 3 + [nc.sync], ts, 0, tab_scales[1])
        load_scale_rows([nc.sync] * 4, ts, 4, tab_scales[0])
        tw1 = load_words(tab_words[1], "tw1")
        b1_t = tile([P, 2, PACK], F32, "b1_t")
        nc.sync.dma_start(b1_t[:], b1.rearrange("(b p t) -> p b t", b=2, t=PACK))
        gain_t = tile([P, 2, PACK], F32, "gain_t")
        nc.sync.dma_start(gain_t[:], gain.rearrange("(b p t) -> p b t", b=2, t=PACK))
        offs3_t = load_list(offs3, "offs3_t")
        page = [tile([P, T2], F32, "page%d" % i) for i in range(8)]
        for i in range(8):
            if i == 1:
                nc.sync.dma_start(w1_raw[1][:], w1_rows[:, :, KP : 2 * KP])
            nc.sync.dma_start(page[i][:], page_rows[i // PACK, i % PACK])
        offs2_t = load_list(offs2, "offs2_t")
        for q in range(4):
            nc.sync.dma_start(
                ts2[32 * q : 32 * q + 8, :].bitcast(I32), tab2_scales[:, 4 * q : 4 * q + 4, :].bitcast(I32)
            )
        t2w = [load_words(tab2_words[a], "t2w%d" % a) for a in range(2)]
        pos1_t = load_list(pos1, "pos1_t")
        pos2_t = load_list(pos2, "pos2_t")
        vis_t = [tile([P, J], F32, "vis%d" % m) for m in range(8)]
        for m in range(8):
            nc.sync.dma_start(vis_t[m][:], vis[P * m : P * (m + 1), :])

        turned = bank(2, "wgs_turned")
        for jb in range(4):
            nc.tensor.transpose(turned[:, P * jb : P * (jb + 1)], wgs_raw[:, P * jb : P * (jb + 1)], identity[:])
        dealt = tile([P, 4, PACK, P], F32, "wgs_dealt")
        nc.vector.tensor_copy(
            dealt[:].rearrange("j b t (r q) -> j b t r q", r=4),
            turned[:].rearrange("j (b q t) -> j b t q", b=4, t=PACK).unsqueeze(3).broadcast_to([P, 4, PACK, 4, 32]),
        )
        backs = []
        for t in range(PACK):
            back = bank(3 + t, "wgs_back%d" % t)
            for jb in range(4):
                nc.tensor.transpose(back[:, P * jb : P * (jb + 1)], dealt[:, jb, t, :], identity[:])
            backs.append(back)

        w4w = tile([P, 2 * H], U8, "w4w")
        nc.vector.tensor_copy(
            w4w[:].rearrange("p (b t q e) -> p b t q e", b=2, t=PACK, e=2),
            w4w_raw[:].rearrange("p (b q t e) -> p b t q e", b=2, t=PACK, e=2),
        )
        w4s = tile([P, H], U8, "w4s")
        nc.vector.tensor_copy(
            w4s[:].rearrange("p (b t q) -> p b t q", b=2, t=PACK),
            w4s_raw[:].rearrange("p (b q t) -> p b t q", b=2, t=PACK),
        )

        def round_w1(b):
            wb = tile([P, PACK * KP], BF16, "w1_bf%d" % b)
            nc.scalar.copy(
                wb[:].rearrange("p (t m j) -> p m t j", t=PACK, j=PACK),
                w1_raw[b][:].rearrange("p j (m t) -> p m t j", t=PACK),
            )
            return wb

        def quantise(src, width, name, tag):
            codes = tile([P, width], U32, name + "_codes", tag)
            plane = tile([P, width], U8, name + "_plane")
            nc.vector.quantize_mx(codes[:].bitcast(FP8X4), plane[:], src)
            return codes, plane

        w1q = [quantise(round_w1(0)[:], KP, "w1q0", None)]
        wg = [tile([P, S], F32, "wg%d" % t) for t in range(PACK)]
        for t in range(PACK):
            nc.scalar.copy(wg[t][:], backs[t][:])

        vw = tile([P, 2, S], U32, "vw")
        vs = tile([P, S], U8, "vs")
        nc.vector.tensor_copy(vw[:, 0, :], tw0[:].bitcast(U32).indirect(offs_t[:]))
        nc.vector.tensor_copy(vs[:], ts[:].indirect(offs_t[:]))
        halves = [slice(0, S // 2), slice(S // 2, S)]

        def entries(lst, js):
            return lst[:, js.start // 16 : js.stop // 16]

        for js in halves:
            nc.vector.tensor_copy(vw[:, 1, js], tw1[:].bitcast(U32).indirect(entries(offs_t, js)))

        def gather_candidate_plane(g, tag):
            cs = tile([P, S], U8, "cs%d" % g, tag)
            nc.vector.tensor_copy(cs[:], ts2[:].indirect(offs2_t[:, 32 * g : 32 * (g + 1)]))
            return cs

        def features(i, put, js, bank_no, sin_tag):
            b, t = divmod(i, PACK)
            x = bank(bank_no, "x%d_%d" % (i, js.start))[:, 0 : js.stop - js.start]
            codes, plane = w1q[b]
            passes = [
                (w4w[:, 2 * P * i : 2 * P * (i + 1)].bitcast(FP4X4), w4s[:, P * i : P * (i + 1)], vw[:, 1, js], vs[:, js]),
                (codes[:, P * t : P * (t + 1)].bitcast(FP8X4), plane[:, P * t : P * (t + 1)], vw[:, 0, js], vs[4:P, js]),
            ]
            if i == 0 and js.start == 0:
                passes = passes[::-1]
            for n, (w_codes, w_plane, v_words, v_plane) in enumerate(passes):
                nc.tensor.matmul_mx(
                    x, lhsT=w_codes, lhsT_scale=w_plane, rhs=v_words.bitcast(FP8X4), rhs_scale=v_plane,
                    start=n == 0, stop=n == 1,
                )
            s = tile([P, js.stop - js.start], F32, "sin%d_%d" % (i, js.start), sin_tag)
            nc.scalar.activation(s[:], x, ACT.Sin, bias=b1_t[:, b, t : t + 1])
            h = tile([P, js.stop - js.start], F32, "h%d_%d" % (i, js.start), "h_%d" % (bank_no % 2))
            if i <= 1:
                nc.scalar.activation(h[:], s[:], ACT.Copy, scale=gain_t[:, b, t : t + 1])
            else:
                nc.gpsimd.tensor_scalar(h[:], s[:], gain_t[:, b, t : t + 1], 0.0, ALU.mult, ALU.add)
            weigher = nc.vector if i == 0 and js.start == 0 else nc.gpsimd
            weigher.tensor_tensor(put[:, js], h[:], wg[t][:, js], ALU.mult)

        def scatter(i, js):
            nc.vector.tensor_copy(page[i][:].indirect(entries(offs3_t, js)), hs[i][:, js])

        whole = slice(0, S)
        hs = [tile([P, S], F32, "h%d" % i) for i in range(8)]
        features(0, hs[0], halves[0], 0, "sin0")
        features(0, hs[0], halves[1], 7, "sin1")
        features(1, hs[1], whole, 1, "sin0")
        features(2, hs[2], whole, 2, "sin1")
        wb1 = round_w1(1)
        features(3, hs[3], whole, 3, "w1_raw1")
        for js in halves:
            scatter(0, js)
        scatter(1, whole)
        w1q.append(quantise(wb1[:], KP, "w1q1", "h1"))
        for i in range(PACK, 8):
            features(i, hs[i], whole, i, "sin%d" % (i % 2))
        for i in range(2, 8):
            scatter(i, whole)

        def round_pairs(a):
            pairs = tile([P, 2, T2, 2], BF16, "pairs%d" % a, "w1_raw%d" % (1 - a))
            for t in range(PACK):
                nc.scalar.copy(pairs[:, t // 2, :, t % 2], page[PACK * a + t][:])
            return pairs[:].rearrange("p u n e -> p (u n e)").bitcast(U32).rearrange("p (u n) -> p n u", u=2)

        def weave(words, n0, width, name):
            woven = tile([P, PACK * width], BF16, name)
            nc.scalar.copy(woven[:].bitcast(U32).rearrange("p (n u) -> p n u", u=2), words[:, n0 : n0 + width, :])
            return woven

        pq0 = quantise(weave(round_pairs(0), 0, T2, "woven0")[:], T2, "pq0", "h6")

        def gather_candidates(g, tag):
            cw = tile([P, 2, S], U32, "cw%d" % g, tag)
            for a in range(2):
                nc.vector.tensor_copy(cw[:, a, :], t2w[a][:].bitcast(U32).indirect(offs2_t[:, 32 * g : 32 * (g + 1)]))
            return cw

        planes = [gather_candidate_plane(0, "h5")]
        cand = [gather_candidates(0, "h7")]
        words1 = round_pairs(1)
        pq1 = [
            quantise(weave(words1, BANK * c, BANK, "woven1_%d" % c)[:], BANK, "pq1_%d" % c, "h%d" % (2 * c))
            for c in range(2)
        ]
        planes.append(gather_candidate_plane(1, "woven1_0"))
        cand.append(gather_candidates(1, "woven1_1"))

        for m in range(8):
            cw, cs = cand[m // 4], planes[m // 4]
            cols = slice(P * (m % 4), P * (m % 4 + 1))
            e = tile([P, T2], F32, "e%d" % m, "e%d" % (m % 3))
            for c in range(2):
                acc = bank(2 * m + c, "acc%d_%d" % (m, c))
                n = slice(BANK * c, BANK * (c + 1))
                nc.tensor.matmul_mx(
                    acc[:], lhsT=cw[:, 1, cols].bitcast(FP8X4), lhsT_scale=cs[4:P, cols],
                    rhs=pq1[c][0][:].bitcast(FP8X4), rhs_scale=pq1[c][1][:], start=True, stop=False,
                )
                nc.tensor.matmul_mx(
                    acc[:], lhsT=cw[:, 0, cols].bitcast(FP8X4), lhsT_scale=cs[:, cols],
                    rhs=pq0[0][:, n].bitcast(FP8X4), rhs_scale=pq0[1][:, n], start=False, stop=True,
                )
                nc.scalar.copy(e[:, n], acc[:])
            first = tile([P, J], F32, "first%d" % m, "first%d" % (m % 2))
            second = tile([P, J], F32, "second%d" % m, "second%d" % (m % 2))
            nc.vector.tensor_copy(first[:], e[:].indirect(pos1_t[:]))
            nc.vector.tensor_copy(second[:], e[:].indirect(pos2_t[:]))
            deeper = tile([P, J], F32, "deeper%d" % m, "deeper%d" % (m % 2))
            nc.vector.tensor_tensor(deeper[:], first[:], second[:], ALU.max)
            res = tile([P, J], F32, "res%d" % m, "res%d" % (m % 3))
            weigher = nc.vector if m == 7 else nc.gpsimd
            weigher.tensor_tensor(res[:], deeper[:], vis_t[m][:], ALU.mult)
            nc.sync.dma_start(out[P * m : P * (m + 1), :], res[:])
